import numpy as np
import ml_dtypes


def mxq(x, axis, fmt="e4m3"):
    dtype, down = {"e4m3": (ml_dtypes.float8_e4m3fn, 7), "e5m2": (ml_dtypes.float8_e5m2, 14)}[fmt]
    v = np.moveaxis(np.asarray(x, np.float32).astype(ml_dtypes.bfloat16).astype(np.float64), axis, -1)
    blocks = v.reshape(v.shape[:-1] + (-1, 32))
    amax = np.abs(blocks).max(-1, keepdims=True)
    byte = np.maximum(np.where(amax > 0, np.frexp(amax)[1] - 1 + 127, 0) - down, 1)
    scale = np.exp2(byte - 127.0)
    codes = (blocks / scale).astype(np.float32).astype(dtype).astype(np.float64)
    return np.moveaxis((codes * scale).reshape(v.shape), -1, axis)


WIDE = False


def mx_kscale(k):
    if not WIDE:
        return np.ones(k)
    levels = np.array([10, -10, 5, -5, 0])
    if k % 512:
        return np.exp2(np.random.permutation(np.resize(levels, k // 32))).repeat(32)
    a = np.empty((k // 512, 16))
    for p in range(k // 512):
        a[p, :8] = np.random.permutation(np.resize(levels, 8))
        for g in range(8):
            far = levels[np.abs(levels - a[p, g]) >= 10]
            a[p, g + 8] = far[np.random.randint(len(far))]
    return np.exp2(a.ravel()).repeat(32)


def f64(x):
    return np.asarray(x).astype(np.float64)


def striped(idx):
    return np.tile(idx.reshape(-1, 16).T, (8, 1)).astype(np.uint16)


def unstriped(offs):
    return offs[:16].T.reshape(-1).astype(np.int64)


K, T, D, S, V, N = 2048, 512, 4, 1024, 256, 128


def setup_inputs():
    n = np.random.standard_normal
    s = mx_kscale(K)[:, None]
    return {
        "xT": (n((K, T)) * s).astype(np.float32),
        "w": (n((K, N)) / np.sqrt(K) / s).astype(np.float32),
        "b": (0.3 * n((N, 1))).astype(np.float32),
        "gate": np.tile(np.random.uniform(0.2, 1.0, (D, 1, V)) / np.sqrt(D), (1, N, 1)).astype(np.float32),
        "pos1": striped(np.random.permutation(T)[:V]),
        "pos2": striped(np.random.permutation(T)[:V]),
        "pos3": striped(np.random.permutation(T)[:V]),
        "pos4": striped(np.random.permutation(T)[:V]),
    }


def reference(xT, w, b, gate, pos1, pos2, pos3, pos4):
    y = mxq(f64(w), 0, "e4m3").T @ mxq(f64(xT), 0, "e4m3")
    y = y + f64(b)
    return sum(f64(gate[d]) * y[:, unstriped(p)] for d, p in enumerate((pos1, pos2, pos3, pos4)))

@@ -1,0 +1,137 @@
+from contextlib import ExitStack
+
+import concourse.mybir as mybir
+
+K, T, D, V, N = 2048, 512, 4, 256, 128
+P = 128
+PACK = 4
+K_PASS = P * PACK
+PASSES = K // K_PASS
+
+FLOPS = 2 * K * T * N + 2 * D * V * N
+
+F32 = mybir.dt.float32
+BF16 = mybir.dt.bfloat16
+U32 = mybir.dt.uint32
+U16 = mybir.dt.uint16
+U8 = mybir.dt.uint8
+FP8X4 = mybir.dt.float8_e4m3fn_x4
+MULT = mybir.AluOpType.mult
+ADD = mybir.AluOpType.add
+IDENTITY = mybir.ActivationFunctionType.Identity
+
+
+def tile_picked_agg_lin_bias_sub_l_kernel(tc, xT, w, b, gate, pos1, pos2, pos3, pos4, out):
+    nc = tc.nc
+    positions = (pos1, pos2, pos3, pos4)
+
+    with ExitStack() as ctx:
+        held = ctx.enter_context(tc.tile_pool(name="held", bufs=1))
+        psum = ctx.enter_context(tc.psum_pool(name="psum", bufs=1))
+
+        lists = [held.tile([P, V // 16], U16, name=f"list{d}") for d in range(D)]
+        gates = [held.tile([P, 2, V], F32, name=f"gates{h}") for h in range(2)]
+        bias = held.tile([P, 1], F32, name="bias")
+        w_raw = held.tile([P, PASSES, PACK, N], F32, name="w_raw")
+        w_grp = held.tile([P, PASSES * N, PACK], BF16, name="w_grp", align_bytes=64)
+        w_codes = held.tile([P, PASSES, N], U32, name="w_codes", align_bytes=64)
+        w_scales = held.tile([P, PASSES, N], U8, name="w_scales", align_bytes=64)
+        x_codes = [held.tile([P, T], U32, name=f"x_codes{g}", align_bytes=64) for g in range(PASSES)]
+        x_scales = [held.tile([P, T], U8, name=f"x_scales{g}", align_bytes=64) for g in range(PASSES)]
+        x_grp = [held.tile([P, T, PACK], BF16, name=f"x_grp{g}", align_bytes=64) for g in range(PASSES)]
+        y = held.tile([P, T], F32, name="y")
+
+        nc.sync.dma_start(out=w_raw[:], in_=w.rearrange("(g p j) m -> p g j m", p=P, j=PACK))
+        cuts = [[(0, 512)], [(0, 512)], [(0, 512)], [(0, 256), (256, 512)]]
+        raws = {}
+        for g in range(PASSES):
+            for c0, c1 in cuts[g]:
+                raw = held.tile([P, PACK, c1 - c0], F32, name=f"x_raw{g}_{c0}")
+                nc.sync.dma_start(out=raw[:], in_=xT[g * K_PASS : (g + 1) * K_PASS, c0:c1].rearrange("(p j) c -> p j c", j=PACK))
+                raws[(g, c0)] = raw
+        nc.sync.dma_start(out=bias[:], in_=b)
+        for h in range(2):
+            for d in (2 * h, 2 * h + 1):
+                nc.sync.dma_start(lists[d][:], positions[d])
+            nc.sync.dma_start(out=gates[h][:], in_=gate[2 * h : 2 * h + 2, :, :].rearrange("d n v -> n d v"))
+
+        def interleave(engine, dst, src):
+            d = dst.rearrange("p (c i) j -> p c j i", i=4)
+            s = src.rearrange("p j (c i) -> p c j i", i=4)
+            if engine == "v":
+                nc.vector.tensor_copy(out=d, in_=s)
+            else:
+                nc.scalar.copy(out=d, in_=s)
+
+        def quantize(codes, scales, grp):
+            nc.vector.quantize_mx(out=codes.bitcast(FP8X4), scales=scales, in_=grp.rearrange("p c j -> p (c j)"))
+
+        for g in range(PASSES):
+            interleave("v" if g < 2 else "s", w_grp[:, g * N : (g + 1) * N, :], w_raw[:, g, :, :])
+        quantize(w_codes[:].rearrange("p g m -> p (g m)"), w_scales[:].rearrange("p g m -> p (g m)"), w_grp[:])
+
+        blocks = [(0, 256), (256, 384), (384, 512)]
+        banks = [psum.tile([P, 512], F32, name=f"bank{i}") for i in range(len(blocks))]
+
+        def product(g, i):
+            c0, c1 = blocks[i]
+            nc.tensor.matmul_mx(
+                out=banks[i][:, 0 : c1 - c0],
+                lhsT=w_codes[:, g, :].bitcast(FP8X4),
+                lhsT_scale=w_scales[:, g, :],
+                rhs=x_codes[g][:, c0:c1].bitcast(FP8X4),
+                rhs_scale=x_scales[g][:, c0:c1],
+                start=(g == 0),
+                stop=(g == PASSES - 1),
+            )
+
+        def emit(i):
+            c0, c1 = blocks[i]
+            nc.scalar.activation(y[:, c0:c1], banks[i][:, 0 : c1 - c0], IDENTITY, bias=bias[:])
+
+        share = 320
+        for g in range(PASSES - 1):
+            raw = raws[(g, 0)]
+            interleave("v", x_grp[g][:, 0:share, :], raw[:, :, 0:share])
+            interleave("s", x_grp[g][:, share:T, :], raw[:, :, share:T])
+            quantize(x_codes[g][:], x_scales[g][:], x_grp[g][:])
+            for i in range(len(blocks)):
+                product(g, i)
+
+        g = PASSES - 1
+        raw = raws[(g, 0)]
+        interleave("v", x_grp[g][:, 0:160, :], raw[:, :, 0:160])
+        interleave("s", x_grp[g][:, 160:256, :], raw[:, :, 160:256])
+        quantize(x_codes[g][:, 0:256], x_scales[g][:, 0:256], x_grp[g][:, 0:256, :])
+        product(g, 0)
+        emit(0)
+        raw = raws[(g, 256)]
+        interleave("v", x_grp[g][:, 256:384, :], raw[:, :, 0:128])
+        interleave("s", x_grp[g][:, 432:512, :], raw[:, :, 176:256])
+        interleave("v", x_grp[g][:, 384:432, :], raw[:, :, 128:176])
+        quantize(x_codes[g][:, 256:384], x_scales[g][:, 256:384], x_grp[g][:, 256:384, :])
+        quantize(x_codes[g][:, 384:512], x_scales[g][:, 384:512], x_grp[g][:, 384:512, :])
+        product(g, 1)
+        product(g, 2)
+        emit(1)
+        emit(2)
+
+        terms = [held.tile([P, V], F32, name=f"term{d}") for d in range(D)]
+
+        def look_up(d):
+            nc.vector.tensor_tensor(terms[d][:], y[:].indirect(lists[d][:]), gates[d // 2][:, d % 2, :], MULT)
+
+        sum01 = held.tile([P, V], F32, name="sum01")
+        sum012 = held.tile([P, V], F32, name="sum012")
+        total = [held.tile([P, V // 2], F32, name=f"total{h}") for h in range(2)]
+        look_up(0)
+        look_up(1)
+        look_up(2)
+        nc.vector.tensor_tensor(sum01[:], terms[0][:], terms[1][:], ADD)
+        look_up(3)
+        halves = [slice(0, V // 2), slice(V // 2, V)]
+        for h in range(2):
+            nc.vector.tensor_tensor(sum012[:, halves[h]], sum01[:, halves[h]], terms[2][:, halves[h]], ADD)
+        for h in range(2):
+            nc.vector.tensor_tensor(total[h][:], sum012[:, halves[h]], terms[3][:, halves[h]], ADD)
+            nc.sync.dma_start(out=out[:, halves[h]], in_=total[h][:])

@@ -41,6 +41,7 @@ def tile_picked_agg_lin_bias_sub_l_kernel(tc, xT, w, b, gate, pos1, pos2, pos3, 
         x_grp = [held.tile([P, T, PACK], BF16, name=f"x_grp{g}", align_bytes=64) for g in range(PASSES)]
         y = held.tile([P, T], F32, name="y")
 
+        nc.scalar.dma_start(out=bias[:], in_=b)
         nc.sync.dma_start(out=w_raw[:], in_=w.rearrange("(g p j) m -> p g j m", p=P, j=PACK))
         cuts = [[(0, 512)], [(0, 512)], [(0, 512)], [(0, 256), (256, 512)]]
         raws = {}
@@ -49,7 +50,6 @@ def tile_picked_agg_lin_bias_sub_l_kernel(tc, xT, w, b, gate, pos1, pos2, pos3, 
                 raw = held.tile([P, PACK, c1 - c0], F32, name=f"x_raw{g}_{c0}")
                 nc.sync.dma_start(out=raw[:], in_=xT[g * K_PASS : (g + 1) * K_PASS, c0:c1].rearrange("(p j) c -> p j c", j=PACK))
                 raws[(g, c0)] = raw
-        nc.sync.dma_start(out=bias[:], in_=b)
         for h in range(2):
             for d in (2 * h, 2 * h + 1):
                 nc.sync.dma_start(lists[d][:], positions[d])
@@ -89,7 +89,7 @@ def tile_picked_agg_lin_bias_sub_l_kernel(tc, xT, w, b, gate, pos1, pos2, pos3, 
             c0, c1 = blocks[i]
             nc.scalar.activation(y[:, c0:c1], banks[i][:, 0 : c1 - c0], IDENTITY, bias=bias[:])
 
-        share = 320
+        share = 224
         for g in range(PASSES - 1):
             raw = raws[(g, 0)]
             interleave("v", x_grp[g][:, 0:share, :], raw[:, :, 0:share])
@@ -104,11 +104,11 @@ def tile_picked_agg_lin_bias_sub_l_kernel(tc, xT, w, b, gate, pos1, pos2, pos3, 
         interleave("s", x_grp[g][:, 160:256, :], raw[:, :, 160:256])
         quantize(x_codes[g][:, 0:256], x_scales[g][:, 0:256], x_grp[g][:, 0:256, :])
         product(g, 0)
-        emit(0)
         raw = raws[(g, 256)]
         interleave("v", x_grp[g][:, 256:384, :], raw[:, :, 0:128])
-        interleave("s", x_grp[g][:, 432:512, :], raw[:, :, 176:256])
-        interleave("v", x_grp[g][:, 384:432, :], raw[:, :, 128:176])
+        interleave("s", x_grp[g][:, 400:512, :], raw[:, :, 144:256])
+        interleave("v", x_grp[g][:, 384:400, :], raw[:, :, 128:144])
+        emit(0)
         quantize(x_codes[g][:, 256:384], x_scales[g][:, 256:384], x_grp[g][:, 256:384, :])
         quantize(x_codes[g][:, 384:512], x_scales[g][:, 384:512], x_grp[g][:, 384:512, :])
         product(g, 1)

from contextlib import ExitStack

import concourse.mybir as mybir

K, T, D, V, N = 2048, 512, 4, 256, 128
P = 128
PACK = 4
K_PASS = P * PACK
PASSES = K // K_PASS

FLOPS = 2 * K * T * N + 2 * D * V * N

F32 = mybir.dt.float32
BF16 = mybir.dt.bfloat16
U32 = mybir.dt.uint32
U16 = mybir.dt.uint16
U8 = mybir.dt.uint8
FP8X4 = mybir.dt.float8_e4m3fn_x4
MULT = mybir.AluOpType.mult
ADD = mybir.AluOpType.add
IDENTITY = mybir.ActivationFunctionType.Identity


def tile_picked_agg_lin_bias_sub_l_kernel(tc, xT, w, b, gate, pos1, pos2, pos3, pos4, out):
    nc = tc.nc
    positions = (pos1, pos2, pos3, pos4)

    with ExitStack() as ctx:
        held = ctx.enter_context(tc.tile_pool(name="held", bufs=1))
        psum = ctx.enter_context(tc.psum_pool(name="psum", bufs=1))

        lists = [held.tile([P, V // 16], U16, name=f"list{d}") for d in range(D)]
        gates = [held.tile([P, 2, V], F32, name=f"gates{h}") for h in range(2)]
        bias = held.tile([P, 1], F32, name="bias")
        w_raw = held.tile([P, PASSES, PACK, N], F32, name="w_raw")
        w_grp = held.tile([P, PASSES * N, PACK], BF16, name="w_grp", align_bytes=64)
        w_codes = held.tile([P, PASSES, N], U32, name="w_codes", align_bytes=64)
        w_scales = held.tile([P, PASSES, N], U8, name="w_scales", align_bytes=64)
        x_codes = [held.tile([P, T], U32, name=f"x_codes{g}", align_bytes=64) for g in range(PASSES)]
        x_scales = [held.tile([P, T], U8, name=f"x_scales{g}", align_bytes=64) for g in range(PASSES)]
        x_grp = [held.tile([P, T, PACK], BF16, name=f"x_grp{g}", align_bytes=64) for g in range(PASSES)]
        y = held.tile([P, T], F32, name="y")

        nc.scalar.dma_start(out=bias[:], in_=b)
        nc.sync.dma_start(out=w_raw[:], in_=w.rearrange("(g p j) m -> p g j m", p=P, j=PACK))
        cuts = [[(0, 512)], [(0, 512)], [(0, 512)], [(0, 256), (256, 512)]]
        raws = {}
        for g in range(PASSES):
            for c0, c1 in cuts[g]:
                raw = held.tile([P, PACK, c1 - c0], F32, name=f"x_raw{g}_{c0}")
                nc.sync.dma_start(out=raw[:], in_=xT[g * K_PASS : (g + 1) * K_PASS, c0:c1].rearrange("(p j) c -> p j c", j=PACK))
                raws[(g, c0)] = raw
        for h in range(2):
            for d in (2 * h, 2 * h + 1):
                nc.sync.dma_start(lists[d][:], positions[d])
            nc.sync.dma_start(out=gates[h][:], in_=gate[2 * h : 2 * h + 2, :, :].rearrange("d n v -> n d v"))

        def interleave(engine, dst, src):
            d = dst.rearrange("p (c i) j -> p c j i", i=4)
            s = src.rearrange("p j (c i) -> p c j i", i=4)
            if engine == "v":
                nc.vector.tensor_copy(out=d, in_=s)
            else:
                nc.scalar.copy(out=d, in_=s)

        def quantize(codes, scales, grp):
            nc.vector.quantize_mx(out=codes.bitcast(FP8X4), scales=scales, in_=grp.rearrange("p c j -> p (c j)"))

        for g in range(PASSES):
            interleave("v" if g < 2 else "s", w_grp[:, g * N : (g + 1) * N, :], w_raw[:, g, :, :])
        quantize(w_codes[:].rearrange("p g m -> p (g m)"), w_scales[:].rearrange("p g m -> p (g m)"), w_grp[:])

        blocks = [(0, 256), (256, 384), (384, 512)]
        banks = [psum.tile([P, 512], F32, name=f"bank{i}") for i in range(len(blocks))]

        def product(g, i):
            c0, c1 = blocks[i]
            nc.tensor.matmul_mx(
                out=banks[i][:, 0 : c1 - c0],
                lhsT=w_codes[:, g, :].bitcast(FP8X4),
                lhsT_scale=w_scales[:, g, :],
                rhs=x_codes[g][:, c0:c1].bitcast(FP8X4),
                rhs_scale=x_scales[g][:, c0:c1],
                start=(g == 0),
                stop=(g == PASSES - 1),
            )

        def emit(i):
            c0, c1 = blocks[i]
            nc.scalar.activation(y[:, c0:c1], banks[i][:, 0 : c1 - c0], IDENTITY, bias=bias[:])

        share = 224
        for g in range(PASSES - 1):
            raw = raws[(g, 0)]
            interleave("v", x_grp[g][:, 0:share, :], raw[:, :, 0:share])
            interleave("s", x_grp[g][:, share:T, :], raw[:, :, share:T])
            quantize(x_codes[g][:], x_scales[g][:], x_grp[g][:])
            for i in range(len(blocks)):
                product(g, i)

        g = PASSES - 1
        raw = raws[(g, 0)]
        interleave("v", x_grp[g][:, 0:160, :], raw[:, :, 0:160])
        interleave("s", x_grp[g][:, 160:256, :], raw[:, :, 160:256])
        quantize(x_codes[g][:, 0:256], x_scales[g][:, 0:256], x_grp[g][:, 0:256, :])
        product(g, 0)
        raw = raws[(g, 256)]
        interleave("v", x_grp[g][:, 256:384, :], raw[:, :, 0:128])
        interleave("s", x_grp[g][:, 400:512, :], raw[:, :, 144:256])
        interleave("v", x_grp[g][:, 384:400, :], raw[:, :, 128:144])
        emit(0)
        quantize(x_codes[g][:, 256:384], x_scales[g][:, 256:384], x_grp[g][:, 256:384, :])
        quantize(x_codes[g][:, 384:512], x_scales[g][:, 384:512], x_grp[g][:, 384:512, :])
        product(g, 1)
        product(g, 2)
        emit(1)
        emit(2)

        terms = [held.tile([P, V], F32, name=f"term{d}") for d in range(D)]

        def look_up(d):
            nc.vector.tensor_tensor(terms[d][:], y[:].indirect(lists[d][:]), gates[d // 2][:, d % 2, :], MULT)

        sum01 = held.tile([P, V], F32, name="sum01")
        sum012 = held.tile([P, V], F32, name="sum012")
        total = [held.tile([P, V // 2], F32, name=f"total{h}") for h in range(2)]
        look_up(0)
        look_up(1)
        look_up(2)
        nc.vector.tensor_tensor(sum01[:], terms[0][:], terms[1][:], ADD)
        look_up(3)
        halves = [slice(0, V // 2), slice(V // 2, V)]
        for h in range(2):
            nc.vector.tensor_tensor(sum012[:, halves[h]], sum01[:, halves[h]], terms[2][:, halves[h]], ADD)
        for h in range(2):
            nc.vector.tensor_tensor(total[h][:], sum012[:, halves[h]], terms[3][:, halves[h]], ADD)
            nc.sync.dma_start(out=out[:, halves[h]], in_=total[h][:])
